import numpy as np
import ml_dtypes


def mxq(x, axis, fmt="e4m3"):
    dtype, down = {"e4m3": (ml_dtypes.float8_e4m3fn, 7), "e5m2": (ml_dtypes.float8_e5m2, 14)}[fmt]
    v = np.moveaxis(np.asarray(x, np.float32).astype(ml_dtypes.bfloat16).astype(np.float64), axis, -1)
    blocks = v.reshape(v.shape[:-1] + (-1, 32))
    amax = np.abs(blocks).max(-1, keepdims=True)
    byte = np.maximum(np.where(amax > 0, np.frexp(amax)[1] - 1 + 127, 0) - down, 1)
    scale = np.exp2(byte - 127.0)
    codes = (blocks / scale).astype(np.float32).astype(dtype).astype(np.float64)
    return np.moveaxis((codes * scale).reshape(v.shape), -1, axis)


WIDE = False


def mx_kscale(k):
    if not WIDE:
        return np.ones(k)
    levels = np.array([10, -10, 5, -5, 0])
    if k % 512:
        return np.exp2(np.random.permutation(np.resize(levels, k // 32))).repeat(32)
    a = np.empty((k // 512, 16))
    for p in range(k // 512):
        a[p, :8] = np.random.permutation(np.resize(levels, 8))
        for g in range(8):
            far = levels[np.abs(levels - a[p, g]) >= 10]
            a[p, g + 8] = far[np.random.randint(len(far))]
    return np.exp2(a.ravel()).repeat(32)


def f64(x):
    return np.asarray(x).astype(np.float64)


def striped(idx):
    return np.tile(idx.reshape(-1, 16).T, (8, 1)).astype(np.uint16)


def unstriped(offs):
    return offs[:16].T.reshape(-1).astype(np.int64)


E2M1 = np.array([0.0, 0.5, 1.0, 1.5, 2.0, 3.0, 4.0, 6.0, -0.0, -0.5, -1.0, -1.5, -2.0, -3.0, -4.0, -6.0])


def pack_weight(w, fmt):
    k, n = w.shape
    w = f64(np.asarray(w, np.float32).astype(ml_dtypes.bfloat16)).reshape(k // 32, 32, n)
    amax = np.abs(w).max(1)
    if fmt == "e4m3":
        byte = np.frexp(amax)[1] - 1 + 127 - 7
    else:
        mant, ex = np.frexp(amax / 6.0)
        byte = np.where(mant > 0.5, ex, ex - 1) + 127
    byte = np.clip(np.where(amax > 0, byte, 1), 1, 254)
    scaled = (w * np.exp2(127.0 - byte)[:, None, :]).reshape(k, n).astype(np.float32)
    by_word = np.ascontiguousarray(scaled.reshape(k // 512, 128, 4, n).transpose(0, 1, 3, 2))
    if fmt == "e4m3":
        words = by_word.astype(ml_dtypes.float8_e4m3fn).view(np.uint8)
    else:
        c = by_word.astype(ml_dtypes.float4_e2m1fn).view(np.uint8) & 0xF
        words = (c[..., 0::2] | (c[..., 1::2] << 4)).reshape(k // 512, 128, 2 * n)
    return np.ascontiguousarray(words), np.ascontiguousarray(byte.astype(np.uint8).reshape(k // 512, 16, n))


def unpack_weight(words, scales, fmt):
    g, _, n = scales.shape
    words = np.ascontiguousarray(words).reshape(g, 128, n, -1)
    if fmt == "e4m3":
        vals = words.view(ml_dtypes.float8_e4m3fn).astype(np.float64)
    else:
        nib = np.empty((g, 128, n, 4), np.uint8)
        nib[..., 0::2] = words & 0xF
        nib[..., 1::2] = words >> 4
        vals = E2M1[nib]
    vals = vals * np.repeat(np.exp2(scales.astype(np.float64) - 127.0), 8, axis=1)[..., None]
    return vals.transpose(0, 1, 3, 2).reshape(g * 512, n)


def gelu(v):
    return 0.5 * v * (1.0 + np.tanh(np.sqrt(2.0 / np.pi) * (v + 0.044715 * v**3)))


K, T, S, H, T2, S2, T3, P = 1024, 2048, 512, 1024, 1024, 1024, 2048, 512

def setup_inputs():
    n = np.random.standard_normal
    s = mx_kscale(K)[:, None]
    u = mx_kscale(H)[:, None]
    tab_words, tab_scales = pack_weight(n((K, T)) * s, "e4m3")
    w2_words, w2_scales = pack_weight(0.6 * n((K, H)) / np.sqrt(K) / s * u.T, "e2m1")
    tab2_words, tab2_scales = pack_weight(n((H, T3)) / np.sqrt(H) / u, "e4m3")
    return {
        "tab_words": tab_words, "tab_scales": tab_scales,
        "offs": striped(np.random.permutation(T)[:S]),
        "w1": (1.6 * n((K, H)) / np.sqrt(K) / s).astype(np.float32),
        "w2_words": w2_words, "w2_scales": w2_scales,
        "wear": (np.exp(0.4 * n((H, S))) * u).astype(np.float32),
        "page0": (n((H, T2)) * u).astype(np.float32),
        "wgs": np.exp(0.3 * n((128, S))).astype(np.float32),
        "offs3": striped(np.random.permutation(T2)[:S]),
        "tab2_words": tab2_words, "tab2_scales": tab2_scales,
        "offs2": striped(np.random.permutation(T3)[:S2]),
        "pos1": striped(np.random.permutation(T2)[:P]),
        "pos2": striped(np.random.permutation(T2)[:P]),
        "bed": (0.6 * n(S2)).astype(np.float32),
    }

def reference(tab_words, tab_scales, offs, w1, w2_words, w2_scales, wear, page0, wgs, offs3,
              tab2_words, tab2_scales, offs2, pos1, pos2, bed):
    v = unpack_weight(tab_words, tab_scales, "e4m3")[:, unstriped(offs)]
    v2 = unpack_weight(tab2_words, tab2_scales, "e4m3")[:, unstriped(offs2)]
    w2 = unpack_weight(w2_words, w2_scales, "e2m1")
    a = mxq(f64(w1), 0, "e4m3").T @ v
    b = w2.T @ v
    h = np.tanh(a) * f64(wear) + b
    page = f64(page0).copy()
    page[:, unstriped(offs3)] = np.tile(f64(wgs), (H // 128, 1)) * h
    e = v2.T @ mxq(page, 0, "e4m3")
    left = e[:, unstriped(pos1)]
    right = e[:, unstriped(pos2)]
    return np.tanh(left - right) * left + f64(bed)[:, None]

@@ -1,0 +1,315 @@
+from contextlib import ExitStack
+
+import concourse.mybir as mybir
+from concourse.masks import make_identity
+
+K, T, S, H, T2, S2, T3, PAIRS = 1024, 2048, 512, 1024, 1024, 1024, 2048, 512
+FLOPS = 2 * K * H * S * 2 + 2 * H * S2 * T2
+
+F32 = mybir.dt.float32
+BF16 = mybir.dt.bfloat16
+I32 = mybir.dt.int32
+U32 = mybir.dt.uint32
+U16 = mybir.dt.uint16
+U8 = mybir.dt.uint8
+FP8X4 = mybir.dt.float8_e4m3fn_x4
+FP4X4 = mybir.dt.float4_e2m1fn_x4
+ACT = mybir.ActivationFunctionType
+ALU = mybir.AluOpType
+
+P = 128
+PACK = 4
+KP = P * PACK
+BANK = 512
+SCALAR_COLS = 192
+
+
+def interleave(engine_copy, grouped, planes, c0, c1):
+    engine_copy(
+        out=grouped[:, c0:c1, :].rearrange("p (c i) t -> p c t i", i=4),
+        in_=planes[:, :, c0:c1].rearrange("p t (c i) -> p c t i", i=4),
+    )
+
+
+def tile_list_potash_face_compare_kernel(
+    tc, tab_words, tab_scales, offs, w1, w2_words, w2_scales, wear, page0, wgs, offs3,
+    tab2_words, tab2_scales, offs2, pos1, pos2, bed, out,
+):
+    nc = tc.nc
+    with ExitStack() as ctx:
+        lists = ctx.enter_context(tc.tile_pool(name="lists", bufs=1))
+        sb = ctx.enter_context(tc.tile_pool(name="sb", bufs=1))
+        ps = ctx.enter_context(tc.psum_pool(name="ps", bufs=1))
+
+        def tile(shape, dtype, name, tag=None):
+            return sb.tile(shape, dtype, name=name, tag=tag or name, align_bytes=64)
+
+        def bank(name, tag):
+            return ps.tile([P, BANK], F32, name=name, tag=tag)
+
+        def load_list(src, name):
+            t = lists.tile([P, src.shape[1]], U16, name=name)
+            nc.sync.dma_start(t[:], src)
+            return t
+
+        def load_table(words, a, name):
+            t = tile([P, T], I32, name, "table%d" % a)
+            nc.sync.dma_start(t[:], words[a].rearrange("p t i -> p (t i)").bitcast(I32))
+            return t
+
+        def load_w1(a, b):
+            t = tile([P, PACK, BANK], F32, "w1_raw%d%d" % (a, b), "raw%d" % (2 * b + a))
+            nc.sync.dma_start(t[:], w1[a * KP:(a + 1) * KP, b * BANK:(b + 1) * BANK].rearrange("(p j) c -> p j c", j=PACK))
+            return t
+
+        def load_w2(b):
+            t = tile([P, 2, 2 * BANK], U8, "w2_%d" % b)
+            for a in range(2):
+                nc.sync.dma_start(t[:, a, :].bitcast(I32), w2_words.bitcast(I32)[a, :, b * 256:(b + 1) * 256])
+            return t
+
+        def load_wear(b):
+            t = tile([P, PACK, S], F32, "wear%d" % b)
+            nc.sync.dma_start(t[:], wear[b * KP:(b + 1) * KP, :].rearrange("(p t) j -> p t j", t=PACK))
+            return t
+
+        def load_page(b, t):
+            pg = tile([P, T2], F32, "page%d%d" % (b, t))
+            nc.sync.dma_start(pg[:], page0[b * KP:(b + 1) * KP, :].rearrange("(p t) n -> t p n", t=PACK)[t])
+            return pg
+
+        wg = tile([P, PACK, S], F32, "wg")
+
+        def load_wgs(t0):
+            src = wgs.rearrange("(q t) j -> q t j", t=PACK)[:, t0:t0 + 2, :]
+            for g in (0, 2, 1, 3):
+                nc.sync.dma_start(wg[32 * g:32 * g + 32, t0:t0 + 2, :], src)
+
+        ts = tile([P, 2, T], U8, "ts")
+        w2s = tile([P, 2, H], U8, "w2s")
+        t2s = tile([P, T3], U8, "t2s")
+        nc.vector.memset(ts[:, 0, :].bitcast(I32), 0)
+        nc.gpsimd.memset(ts[:, 1, :].bitcast(I32), 0)
+        nc.vector.memset(w2s[:].bitcast(I32), 0)
+        nc.gpsimd.memset(t2s[:].bitcast(I32), 0)
+        ident = tile([P, P], F32, "ident")
+        make_identity(nc, ident[:])
+
+        offs_t = load_list(offs, "offs_t")
+        offs3_t = load_list(offs3, "offs3_t")
+        offs2_t = load_list(offs2, "offs2_t")
+        pos1_t = load_list(pos1, "pos1_t")
+        pos2_t = load_list(pos2, "pos2_t")
+        tab = [load_table(tab_words, 0, "tab0")]
+        for q in range(4):
+            nc.sync.dma_start(
+                ts[32 * q:32 * q + 4, :, :].bitcast(I32),
+                tab_scales.bitcast(I32)[:, 4 * q:4 * q + 4, :].rearrange("a r t -> r a t"))
+        tab.append(load_table(tab_words, 1, "tab1"))
+        w2t = {0: load_w2(0)}
+        raw = {(0, 0): load_w1(0, 0)}
+        for q in range(4):
+            nc.sync.dma_start(
+                w2s[32 * q:32 * q + 4, :, :].bitcast(I32),
+                w2_scales.bitcast(I32)[:, 4 * q:4 * q + 4, :].rearrange("a r t -> r a t"))
+        raw[1, 0] = load_w1(1, 0)
+        for q in range(4):
+            nc.sync.dma_start(
+                t2s[32 * q:32 * q + 8, :].bitcast(I32),
+                tab2_scales.bitcast(I32)[:, 4 * q:4 * q + 4, :])
+        weart = {0: load_wear(0)}
+        page = {(0, 0): load_page(0, 0)}
+        load_wgs(0)
+        raw[0, 1] = load_w1(0, 1)
+        page[0, 1] = load_page(0, 1)
+        raw[1, 1] = load_w1(1, 1)
+        page[0, 2] = load_page(0, 2)
+        load_wgs(2)
+        w2t[1] = load_w2(1)
+        weart[1] = load_wear(1)
+        page[0, 3] = load_page(0, 3)
+        for t in range(PACK):
+            page[1, t] = load_page(1, t)
+
+        vc, vs = [], []
+        for a in range(2):
+            c = tile([P, S], U32, "vc%d" % a)
+            nc.vector.tensor_copy(c[:], tab[a][:].bitcast(U32).indirect(offs_t[:]))
+            s = tile([P, S], U8, "vs%d" % a)
+            nc.vector.tensor_copy(s[:], ts[:, a, :].indirect(offs_t[:]))
+            vc.append(c)
+            vs.append(s)
+
+        tab2 = [load_table(tab2_words, a, "tab2_%d" % a) for a in range(2)]
+        bed_t = tile([P, S2 // P], F32, "bed_t")
+        with nc.allow_non_contiguous_dma(reason="one value of bed to each partition and row tile"):
+            nc.sync.dma_start(bed_t[:], bed.rearrange("(i p) -> p i", p=P))
+
+        w1c, w1s, bT, t2T, hh = {}, {}, {}, {}, {}
+
+        def quantise_w1(a, b, scalar_cols):
+            grp = tile([P, BANK, PACK], BF16, "grp%d%d" % (a, b), "grp%d" % a)
+            if scalar_cols > 0:
+                interleave(nc.scalar.copy, grp, raw[a, b], 0, scalar_cols)
+            if scalar_cols < BANK:
+                interleave(nc.vector.tensor_copy, grp, raw[a, b], scalar_cols, BANK)
+            w1c[a, b] = tile([P, BANK], U32, "w1c%d%d" % (a, b))
+            w1s[a, b] = tile([P, BANK], U8, "w1s%d%d" % (a, b))
+            nc.vector.quantize_mx(out=w1c[a, b][:].bitcast(FP8X4), scales=w1s[a, b][:],
+                                  in_=grp[:].rearrange("p c t -> p (c t)"))
+
+        def plain_part(b, jb):
+            cols = slice(jb * P, (jb + 1) * P)
+            acc = bank("B%d%d" % (b, jb), "B%d" % (jb % 2))
+            for a in range(2):
+                nc.tensor.matmul_mx(
+                    out=acc[:], lhsT=vc[a][:, cols].bitcast(FP8X4), lhsT_scale=vs[a][:, cols],
+                    rhs=w2t[b][:, a, :].bitcast(FP4X4), rhs_scale=w2s[:, a, b * BANK:(b + 1) * BANK],
+                    start=(a == 0), stop=(a == 1))
+            bT[b, jb] = tile([P, PACK, P], F32, "bT%d%d" % (b, jb), "u%d" % (8 * b + jb))
+            nc.scalar.copy(out=bT[b, jb][:], in_=acc[:].rearrange("j (p t) -> j t p", t=PACK))
+
+        accA = {}
+
+        def w1_pass(b, jb, a):
+            cols = slice(jb * P, (jb + 1) * P)
+            if a == 0:
+                accA[b, jb] = bank("A%d%d" % (b, jb), (("A0", "A1", "H0", "H1"), ("A0", "A1", "A0", "A1"))[b][jb])
+            nc.tensor.matmul_mx(
+                out=accA[b, jb][:], lhsT=vc[a][:, cols].bitcast(FP8X4), lhsT_scale=vs[a][:, cols],
+                rhs=w1c[a, b][:].bitcast(FP8X4), rhs_scale=w1s[a, b][:],
+                start=(a == 0), stop=(a == 1))
+
+        def bounded_part(b, jb):
+            cols = slice(jb * P, (jb + 1) * P)
+            acc = accA[b, jb]
+            t1 = tile([P, PACK, P], F32, "t1_%d%d" % (b, jb), "t1_%d" % jb)
+            nc.scalar.activation(out=t1[:], in_=acc[:].rearrange("j (p t) -> j t p", t=PACK), func=ACT.Tanh)
+            wT = bank("W%d%d" % (b, jb), (("W0", "W1", "B0", "B1"), ("W0", "W1", "W0", "W1"))[b][jb])
+            for t in range(PACK):
+                nc.tensor.transpose(wT[:, t * P:(t + 1) * P], weart[b][:, t, cols], ident[:])
+            t2T[b, jb] = tile([P, PACK, P], F32, "t2_%d%d" % (b, jb), "u%d" % (8 * b + 4 + jb))
+            nc.vector.tensor_tensor(t2T[b, jb][:].rearrange("j t p -> j (t p)"),
+                                    t1[:].rearrange("j t p -> j (t p)"), wT[:], ALU.mult)
+
+        def make_h(b, t, bank_tag, h_tag):
+            acc = bank("H%d%d" % (b, t), bank_tag)
+            for jb in range(4):
+                cols = slice(jb * P, (jb + 1) * P)
+                nc.tensor.matmul(acc[:, cols], lhsT=bT[b, jb][:, t, :], rhs=ident[:],
+                                 is_transpose=True, start=True, stop=False)
+                nc.tensor.matmul(acc[:, cols], lhsT=t2T[b, jb][:, t, :], rhs=ident[:],
+                                 is_transpose=True, start=False, stop=True)
+            hh[b, t] = tile([P, S], F32, "h%d%d" % (b, t), h_tag)
+            nc.scalar.copy(out=hh[b, t][:], in_=acc[:])
+
+        planes = {}
+
+        def scatter(b, t):
+            nc.vector.tensor_tensor(page[b, t][:].indirect(offs3_t[:]), hh[b, t][:], wg[:, t, :], ALU.mult)
+            for nh in range(2):
+                if t == 0:
+                    planes[b, nh] = tile([P, PACK, BANK], F32, "planes%d%d" % (b, nh))
+                if (b, t) != (1, 3):
+                    nc.sync.dma_start(planes[b, nh][:, t, :], page[b, t][:, nh * BANK:(nh + 1) * BANK])
+
+        pgrp, pc, psc = {}, {}, {}
+
+        def quantise_page(a, nh):
+            if nh == 0:
+                pgrp[a] = tile([P, T2, PACK], BF16, "pgrp%d" % a, "wear%d" % a)
+            grp = pgrp[a][:, nh * BANK:(nh + 1) * BANK, :]
+            interleave(nc.scalar.copy, grp, planes[a, nh], 0, BANK)
+            pc[a, nh] = tile([P, BANK], U32, "pc%d%d" % (a, nh))
+            psc[a, nh] = tile([P, BANK], U8, "psc%d%d" % (a, nh))
+            nc.vector.quantize_mx(out=pc[a, nh][:].bitcast(FP8X4), scales=psc[a, nh][:],
+                                  in_=grp.rearrange("p c t -> p (c t)"))
+
+        for jb in range(4):
+            plain_part(0, jb)
+        quantise_w1(0, 0, 0)
+        for jb in range(4):
+            w1_pass(0, jb, 0)
+        quantise_w1(1, 0, SCALAR_COLS)
+        for jb in range(4):
+            w1_pass(0, jb, 1)
+            bounded_part(0, jb)
+        make_h(0, 0, "A0", "h0")
+        scatter(0, 0)
+        make_h(0, 1, "A1", "h1")
+        scatter(0, 1)
+        v2s = tile([P, S2], U8, "v2s")
+        for nh in range(2):
+            nc.vector.tensor_copy(v2s[:, nh * 512:(nh + 1) * 512], t2s[:].indirect(offs2_t[:, nh * 32:(nh + 1) * 32]))
+        quantise_w1(0, 1, BANK)
+        quantise_w1(1, 1, BANK)
+        make_h(0, 2, "H0", "raw3")
+        scatter(0, 2)
+        for jb in range(4):
+            plain_part(1, jb)
+        for jb in range(4):
+            w1_pass(1, jb, 0)
+            w1_pass(1, jb, 1)
+            bounded_part(1, jb)
+        make_h(0, 3, "A0", "h2")
+        scatter(0, 3)
+        make_h(1, 0, "H1", "h0")
+        scatter(1, 0)
+        make_h(1, 1, "H0", "h1")
+        scatter(1, 1)
+        make_h(1, 2, "H1", "h2")
+        scatter(1, 2)
+        quantise_page(0, 0)
+        make_h(1, 3, "H0", "planes00")
+        quantise_page(0, 1)
+        scatter(1, 3)
+
+        v2c = tile([P, 2, S2], U32, "v2c", "wg")
+        for nh in range(2):
+            nc.vector.tensor_copy(out=planes[1, nh][:, 3, :], in_=page[1, 3][:, nh * BANK:(nh + 1) * BANK])
+        for nh in range(2):
+            for a in range(2):
+                nc.vector.tensor_copy(
+                    v2c[:, a, nh * 512:(nh + 1) * 512],
+                    tab2[a][:].bitcast(U32).indirect(offs2_t[:, nh * 32:(nh + 1) * 32]))
+            quantise_page(1, nh)
+
+        bank_tags = ("B0", "B1", "W0", "W1", "A0", "A1", "H1", "H0")
+        e, left, th = {}, {}, {}
+
+        def scores(i):
+            rows = slice(i * P, (i + 1) * P)
+            e[i] = tile([P, T2], F32, "e%d" % i, "raw%d" % (i % 3))
+            for nh in range(2):
+                acc = bank("E%d%d" % (i, nh), bank_tags[(2 * i + nh) % 8])
+                for a in range(2):
+                    nc.tensor.matmul_mx(
+                        out=acc[:], lhsT=v2c[:, a, rows].bitcast(FP8X4), lhsT_scale=v2s[4 * a:P, rows],
+                        rhs=pc[a, nh][:].bitcast(FP8X4), rhs_scale=psc[a, nh][:],
+                        start=(a == 0), stop=(a == 1))
+                nc.scalar.copy(out=e[i][:, nh * BANK:(nh + 1) * BANK], in_=acc[:])
+
+        def pick(i):
+            left[i] = tile([P, PAIRS], F32, "left%d" % i, "u%d" % (i % 3))
+            nc.vector.tensor_copy(left[i][:], e[i][:].indirect(pos1_t[:]))
+            diff = tile([P, PAIRS], F32, "diff%d" % i, "u%d" % (3 + i % 2))
+            nc.vector.tensor_tensor(diff[:], e[i][:].indirect(pos2_t[:]), left[i][:], ALU.subtract)
+            th[i] = tile([P, PAIRS], F32, "th%d" % i, "u%d" % (5 + i % 2))
+            nc.scalar.activation(out=th[i][:], in_=diff[:], func=ACT.Tanh, scale=-1.0)
+
+        def finish(i):
+            prod = tile([P, PAIRS], F32, "prod%d" % i, "u%d" % (7 + i % 2))
+            nc.vector.tensor_tensor(prod[:], th[i][:], left[i][:], ALU.mult)
+            res = tile([P, PAIRS], F32, "res%d" % i, "u%d" % (9 + i % 3))
+            nc.scalar.activation(out=res[:], in_=prod[:], func=ACT.Identity, bias=bed_t[:, i:i + 1])
+            nc.sync.dma_start(out[i * P:(i + 1) * P, :], res[:])
+
+        n_tiles = S2 // P
+        scores(0)
+        for i in range(n_tiles):
+            if i + 1 < n_tiles:
+                scores(i + 1)
+            pick(i)
+            if i > 0:
+                finish(i - 1)
+        finish(n_tiles - 1)

@@ -21,7 +21,10 @@ P = 128
 PACK = 4
 KP = P * PACK
 BANK = 512
-SCALAR_COLS = 192
+PIECE = 128
+SUB_TILES = 6
+MUL_TILES = 4
+LAST_SCALAR_COLS = 640
 
 
 def interleave(engine_copy, grouped, planes, c0, c1):
@@ -39,6 +42,7 @@ def tile_list_potash_face_compare_kernel(
     with ExitStack() as ctx:
         lists = ctx.enter_context(tc.tile_pool(name="lists", bufs=1))
         sb = ctx.enter_context(tc.tile_pool(name="sb", bufs=1))
+        late = ctx.enter_context(tc.tile_pool(name="late", bufs=1))
         ps = ctx.enter_context(tc.psum_pool(name="ps", bufs=1))
 
         def tile(shape, dtype, name, tag=None):
@@ -57,20 +61,26 @@ def tile_list_potash_face_compare_kernel(
             nc.sync.dma_start(t[:], words[a].rearrange("p t i -> p (t i)").bitcast(I32))
             return t
 
-        def load_w1(a, b):
-            t = tile([P, PACK, BANK], F32, "w1_raw%d%d" % (a, b), "raw%d" % (2 * b + a))
-            nc.sync.dma_start(t[:], w1[a * KP:(a + 1) * KP, b * BANK:(b + 1) * BANK].rearrange("(p j) c -> p j c", j=PACK))
-            return t
+        def load_w1(a, b, pieces=1):
+            src = w1[a * KP:(a + 1) * KP, b * BANK:(b + 1) * BANK].rearrange("(p j) c -> p j c", j=PACK)
+            width = BANK // pieces
+            tiles = []
+            for n in range(pieces):
+                t = tile([P, PACK, width], F32, "w1_raw%d%d%d" % (a, b, n), "raw%d" % (2 * b + a + 4 * n))
+                nc.sync.dma_start(t[:], src[:, :, n * width:(n + 1) * width])
+                tiles.append(t)
+            return tiles
 
         def load_w2(b):
             t = tile([P, 2, 2 * BANK], U8, "w2_%d" % b)
-            for a in range(2):
-                nc.sync.dma_start(t[:, a, :].bitcast(I32), w2_words.bitcast(I32)[a, :, b * 256:(b + 1) * 256])
+            src = w2_words.bitcast(I32)[:, :, b * 256:(b + 1) * 256].rearrange("a p c -> p a c")
+            nc.sync.dma_start(t[:].bitcast(I32), src)
             return t
 
-        def load_wear(b):
-            t = tile([P, PACK, S], F32, "wear%d" % b)
-            nc.sync.dma_start(t[:], wear[b * KP:(b + 1) * KP, :].rearrange("(p t) j -> p t j", t=PACK))
+        def load_wear(b, jh):
+            t = tile([P, PACK, S // 2], F32, "wear%d%d" % (b, jh))
+            src = wear[b * KP:(b + 1) * KP, jh * (S // 2):(jh + 1) * (S // 2)]
+            nc.sync.dma_start(t[:], src.rearrange("(p t) j -> p t j", t=PACK))
             return t
 
         def load_page(b, t):
@@ -80,18 +90,21 @@ def tile_list_potash_face_compare_kernel(
 
         wg = tile([P, PACK, S], F32, "wg")
 
-        def load_wgs(t0):
-            src = wgs.rearrange("(q t) j -> q t j", t=PACK)[:, t0:t0 + 2, :]
+        def load_wgs(t0, t1):
+            src = wgs.rearrange("(q t) j -> q t j", t=PACK)[:, t0:t1, :]
             for g in (0, 2, 1, 3):
-                nc.sync.dma_start(wg[32 * g:32 * g + 32, t0:t0 + 2, :], src)
+                nc.sync.dma_start(wg[32 * g:32 * g + 32, t0:t1, :], src)
 
         ts = tile([P, 2, T], U8, "ts")
         w2s = tile([P, 2, H], U8, "w2s")
         t2s = tile([P, T3], U8, "t2s")
-        nc.vector.memset(ts[:, 0, :].bitcast(I32), 0)
-        nc.gpsimd.memset(ts[:, 1, :].bitcast(I32), 0)
-        nc.vector.memset(w2s[:].bitcast(I32), 0)
-        nc.gpsimd.memset(t2s[:].bitcast(I32), 0)
+        nc.vector.memset(ts[:].bitcast(I32), 0)
+        nc.vector.memset(t2s[:].bitcast(I32), 0)
+        nc.gpsimd.memset(w2s[:].bitcast(I32), 0)
+        for q in range(4):
+            nc.gpsimd.dma_start(
+                w2s[32 * q:32 * q + 4, :, :].bitcast(I32),
+                w2_scales.bitcast(I32)[:, 4 * q:4 * q + 4, :].rearrange("a r t -> r a t"))
         ident = tile([P, P], F32, "ident")
         make_identity(nc, ident[:])
 
@@ -100,34 +113,32 @@ def tile_list_potash_face_compare_kernel(
         offs2_t = load_list(offs2, "offs2_t")
         pos1_t = load_list(pos1, "pos1_t")
         pos2_t = load_list(pos2, "pos2_t")
-        tab = [load_table(tab_words, 0, "tab0")]
+        tab = [load_table(tab_words, a, "tab%d" % a) for a in range(2)]
+        w2t = {0: load_w2(0)}
         for q in range(4):
             nc.sync.dma_start(
                 ts[32 * q:32 * q + 4, :, :].bitcast(I32),
                 tab_scales.bitcast(I32)[:, 4 * q:4 * q + 4, :].rearrange("a r t -> r a t"))
-        tab.append(load_table(tab_words, 1, "tab1"))
-        w2t = {0: load_w2(0)}
         raw = {(0, 0): load_w1(0, 0)}
-        for q in range(4):
-            nc.sync.dma_start(
-                w2s[32 * q:32 * q + 4, :, :].bitcast(I32),
-                w2_scales.bitcast(I32)[:, 4 * q:4 * q + 4, :].rearrange("a r t -> r a t"))
-        raw[1, 0] = load_w1(1, 0)
         for q in range(4):
             nc.sync.dma_start(
                 t2s[32 * q:32 * q + 8, :].bitcast(I32),
                 tab2_scales.bitcast(I32)[:, 4 * q:4 * q + 4, :])
-        weart = {0: load_wear(0)}
-        page = {(0, 0): load_page(0, 0)}
-        load_wgs(0)
+        raw[1, 0] = load_w1(1, 0, 2)
+        weart = {(0, jh): load_wear(0, jh) for jh in range(2)}
         raw[0, 1] = load_w1(0, 1)
+        page = {(0, 0): load_page(0, 0)}
+        load_wgs(0, 1)
         page[0, 1] = load_page(0, 1)
+        load_wgs(1, 2)
         raw[1, 1] = load_w1(1, 1)
-        page[0, 2] = load_page(0, 2)
-        load_wgs(2)
         w2t[1] = load_w2(1)
-        weart[1] = load_wear(1)
+        page[0, 2] = load_page(0, 2)
+        load_wgs(2, 3)
+        for jh in range(2):
+            weart[1, jh] = load_wear(1, jh)
         page[0, 3] = load_page(0, 3)
+        load_wgs(3, 4)
         for t in range(PACK):
             page[1, t] = load_page(1, t)
 
@@ -140,19 +151,17 @@ def tile_list_potash_face_compare_kernel(
             vc.append(c)
             vs.append(s)
 
-        tab2 = [load_table(tab2_words, a, "tab2_%d" % a) for a in range(2)]
         bed_t = tile([P, S2 // P], F32, "bed_t")
         with nc.allow_non_contiguous_dma(reason="one value of bed to each partition and row tile"):
             nc.sync.dma_start(bed_t[:], bed.rearrange("(i p) -> p i", p=P))
 
         w1c, w1s, bT, t2T, hh = {}, {}, {}, {}, {}
 
-        def quantise_w1(a, b, scalar_cols):
-            grp = tile([P, BANK, PACK], BF16, "grp%d%d" % (a, b), "grp%d" % a)
-            if scalar_cols > 0:
-                interleave(nc.scalar.copy, grp, raw[a, b], 0, scalar_cols)
-            if scalar_cols < BANK:
-                interleave(nc.vector.tensor_copy, grp, raw[a, b], scalar_cols, BANK)
+        def quantise_w1(a, b, engine_copy, piece, grp):
+            width = BANK // len(raw[a, b])
+            for n, src in enumerate(raw[a, b]):
+                for c0 in range(0, width, piece):
+                    interleave(engine_copy, grp[:, n * width:(n + 1) * width, :], src, c0, c0 + piece)
             w1c[a, b] = tile([P, BANK], U32, "w1c%d%d" % (a, b))
             w1s[a, b] = tile([P, BANK], U8, "w1s%d%d" % (a, b))
             nc.vector.quantize_mx(out=w1c[a, b][:].bitcast(FP8X4), scales=w1s[a, b][:],
@@ -160,7 +169,7 @@ def tile_list_potash_face_compare_kernel(
 
         def plain_part(b, jb):
             cols = slice(jb * P, (jb + 1) * P)
-            acc = bank("B%d%d" % (b, jb), "B%d" % (jb % 2))
+            acc = bank("B%d%d" % (b, jb), (("B0", "B1", "W0", "W1"), ("W0", "W1", "A0", "A1"))[b][jb])
             for a in range(2):
                 nc.tensor.matmul_mx(
                     out=acc[:], lhsT=vc[a][:, cols].bitcast(FP8X4), lhsT_scale=vs[a][:, cols],
@@ -174,23 +183,29 @@ def tile_list_potash_face_compare_kernel(
         def w1_pass(b, jb, a):
             cols = slice(jb * P, (jb + 1) * P)
             if a == 0:
-                accA[b, jb] = bank("A%d%d" % (b, jb), (("A0", "A1", "H0", "H1"), ("A0", "A1", "A0", "A1"))[b][jb])
+                accA[b, jb] = bank("A%d%d" % (b, jb), (("A0", "A1", "H0", "H1"), ("B0", "B1", "H1", "H0"))[b][jb])
             nc.tensor.matmul_mx(
                 out=accA[b, jb][:], lhsT=vc[a][:, cols].bitcast(FP8X4), lhsT_scale=vs[a][:, cols],
                 rhs=w1c[a, b][:].bitcast(FP8X4), rhs_scale=w1s[a, b][:],
                 start=(a == 0), stop=(a == 1))
 
-        def bounded_part(b, jb):
-            cols = slice(jb * P, (jb + 1) * P)
-            acc = accA[b, jb]
-            t1 = tile([P, PACK, P], F32, "t1_%d%d" % (b, jb), "t1_%d" % jb)
-            nc.scalar.activation(out=t1[:], in_=acc[:].rearrange("j (p t) -> j t p", t=PACK), func=ACT.Tanh)
-            wT = bank("W%d%d" % (b, jb), (("W0", "W1", "B0", "B1"), ("W0", "W1", "W0", "W1"))[b][jb])
+        wT = {}
+
+        def turn_wear(b, jb):
+            wT[b, jb] = bank("W%d%d" % (b, jb), (("B0", "B1", "W0", "W1"), ("W0", "W1", "A0", "A1"))[b][jb])
             for t in range(PACK):
-                nc.tensor.transpose(wT[:, t * P:(t + 1) * P], weart[b][:, t, cols], ident[:])
+                nc.tensor.transpose(wT[b, jb][:, t * P:(t + 1) * P],
+                                    weart[b, jb // 2][:, t, jb % 2 * P:(jb % 2 + 1) * P], ident[:])
+
+        def bounded_part(b, jb):
+            if (b, jb) == (0, 3):
+                t1 = late.tile([P, PACK, P], F32, name="t1_03", offset=0, align_bytes=64)
+            else:
+                t1 = tile([P, PACK, P], F32, "t1_%d%d" % (b, jb), "t1_%d" % jb)
+            nc.scalar.activation(out=t1[:], in_=accA[b, jb][:].rearrange("j (p t) -> j t p", t=PACK), func=ACT.Tanh)
             t2T[b, jb] = tile([P, PACK, P], F32, "t2_%d%d" % (b, jb), "u%d" % (8 * b + 4 + jb))
             nc.vector.tensor_tensor(t2T[b, jb][:].rearrange("j t p -> j (t p)"),
-                                    t1[:].rearrange("j t p -> j (t p)"), wT[:], ALU.mult)
+                                    t1[:].rearrange("j t p -> j (t p)"), wT[b, jb][:], ALU.mult)
 
         def make_h(b, t, bank_tag, h_tag):
             acc = bank("H%d%d" % (b, t), bank_tag)
@@ -215,93 +230,122 @@ def tile_list_potash_face_compare_kernel(
 
         pgrp, pc, psc = {}, {}, {}
 
-        def quantise_page(a, nh):
-            if nh == 0:
-                pgrp[a] = tile([P, T2, PACK], BF16, "pgrp%d" % a, "wear%d" % a)
-            grp = pgrp[a][:, nh * BANK:(nh + 1) * BANK, :]
-            interleave(nc.scalar.copy, grp, planes[a, nh], 0, BANK)
-            pc[a, nh] = tile([P, BANK], U32, "pc%d%d" % (a, nh))
-            psc[a, nh] = tile([P, BANK], U8, "psc%d%d" % (a, nh))
-            nc.vector.quantize_mx(out=pc[a, nh][:].bitcast(FP8X4), scales=psc[a, nh][:],
-                                  in_=grp.rearrange("p c t -> p (c t)"))
+        def round_page(a, nh, engine_copy, c0, c1):
+            interleave(engine_copy, pgrp[a][:, nh * BANK:(nh + 1) * BANK, :], planes[a, nh], c0, c1)
 
+        def quantise_page(a):
+            pc[a] = tile([P, T2], U32, "pc%d" % a, "wear%d1" % a)
+            psc[a] = tile([P, T2], U8, "psc%d" % a)
+            nc.vector.quantize_mx(out=pc[a][:].bitcast(FP8X4), scales=psc[a][:],
+                                  in_=pgrp[a][:].rearrange("p c t -> p (c t)"))
+
+        v2c, v2s = {}, {}
+
+        def gather_v2_scales(half, dst):
+            v2s[half] = dst
+            nc.vector.tensor_copy(v2s[half][:], t2s[:].indirect(offs2_t[:, half * 32:(half + 1) * 32]))
+
+        def gather_v2_words(half, tag):
+            v2c[half] = tile([P, 2, 512], U32, "v2c%d" % half, tag)
+            for a in range(2):
+                nc.vector.tensor_copy(
+                    v2c[half][:, a, :], tab2[a][:].bitcast(U32).indirect(offs2_t[:, half * 32:(half + 1) * 32]))
+
+        quantise_w1(0, 0, nc.vector.tensor_copy, BANK, tile([P, BANK, PACK], BF16, "grp00", "grp0"))
+        quantise_w1(1, 0, nc.vector.tensor_copy, BANK // 2, tile([P, BANK, PACK], BF16, "grp10", "grp1"))
         for jb in range(4):
             plain_part(0, jb)
-        quantise_w1(0, 0, 0)
         for jb in range(4):
             w1_pass(0, jb, 0)
-        quantise_w1(1, 0, SCALAR_COLS)
+        gather_v2_scales(0, tile([P, 512], U8, "v2s0", "grp1"))
+        turn_wear(0, 0)
+        turn_wear(0, 1)
         for jb in range(4):
             w1_pass(0, jb, 1)
+        turn_wear(0, 2)
+        turn_wear(0, 3)
+        for jb in range(4):
             bounded_part(0, jb)
+        gather_v2_scales(1, late.tile([P, 512], U8, name="v2s1", offset=0, align_bytes=64))
         make_h(0, 0, "A0", "h0")
         scatter(0, 0)
-        make_h(0, 1, "A1", "h1")
+        quantise_w1(0, 1, nc.scalar.copy, PIECE, late.tile([P, BANK, PACK], BF16, name="grp01", offset=512, align_bytes=64))
+        make_h(0, 1, "A1", "raw2")
         scatter(0, 1)
-        v2s = tile([P, S2], U8, "v2s")
-        for nh in range(2):
-            nc.vector.tensor_copy(v2s[:, nh * 512:(nh + 1) * 512], t2s[:].indirect(offs2_t[:, nh * 32:(nh + 1) * 32]))
-        quantise_w1(0, 1, BANK)
-        quantise_w1(1, 1, BANK)
+        quantise_w1(1, 1, nc.scalar.copy, PIECE, tile([P, BANK, PACK], BF16, "grp11", "grp0"))
         make_h(0, 2, "H0", "raw3")
         scatter(0, 2)
         for jb in range(4):
             plain_part(1, jb)
         for jb in range(4):
             w1_pass(1, jb, 0)
+        for jb in range(4):
             w1_pass(1, jb, 1)
+        for jb in range(4):
+            turn_wear(1, jb)
             bounded_part(1, jb)
-        make_h(0, 3, "A0", "h2")
+        make_h(0, 3, "H1", "table0")
         scatter(0, 3)
-        make_h(1, 0, "H1", "h0")
+        tab2 = [load_table(tab2_words, 0, "tab2_0")]
+        make_h(1, 0, "A1", "table1")
         scatter(1, 0)
-        make_h(1, 1, "H0", "h1")
+        tab2.append(load_table(tab2_words, 1, "tab2_1"))
+        make_h(1, 1, "A0", "h0")
         scatter(1, 1)
-        make_h(1, 2, "H1", "h2")
+        make_h(1, 2, "H0", "h1")
         scatter(1, 2)
-        quantise_page(0, 0)
-        make_h(1, 3, "H0", "planes00")
-        quantise_page(0, 1)
+        pgrp[0] = tile([P, T2, PACK], BF16, "pgrp0", "wear00")
+        round_page(0, 0, nc.scalar.copy, 0, BANK)
+        make_h(1, 3, "H1", "planes00")
+        round_page(0, 1, nc.scalar.copy, 0, BANK)
+        quantise_page(0)
         scatter(1, 3)
 
-        v2c = tile([P, 2, S2], U32, "v2c", "wg")
+        pgrp[1] = tile([P, T2, PACK], BF16, "pgrp1", "wear10")
         for nh in range(2):
             nc.vector.tensor_copy(out=planes[1, nh][:, 3, :], in_=page[1, 3][:, nh * BANK:(nh + 1) * BANK])
-        for nh in range(2):
-            for a in range(2):
-                nc.vector.tensor_copy(
-                    v2c[:, a, nh * 512:(nh + 1) * 512],
-                    tab2[a][:].bitcast(U32).indirect(offs2_t[:, nh * 32:(nh + 1) * 32]))
-            quantise_page(1, nh)
+        round_page(1, 0, nc.scalar.copy, 0, BANK)
+        round_page(1, 1, nc.scalar.copy, 0, LAST_SCALAR_COLS - BANK)
+        round_page(1, 1, nc.vector.tensor_copy, LAST_SCALAR_COLS - BANK, BANK)
+        gather_v2_words(0, "wg")
+        quantise_page(1)
+        gather_v2_words(1, "wear10")
 
         bank_tags = ("B0", "B1", "W0", "W1", "A0", "A1", "H1", "H0")
-        e, left, th = {}, {}, {}
+        e, left, right, th = {}, {}, {}, {}
 
         def scores(i):
-            rows = slice(i * P, (i + 1) * P)
-            e[i] = tile([P, T2], F32, "e%d" % i, "raw%d" % (i % 3))
+            half, rows = i // 4, slice(i % 4 * P, (i % 4 + 1) * P)
+            e[i] = tile([P, T2], F32, "e%d" % i, "raw%d" % (i % 4))
             for nh in range(2):
                 acc = bank("E%d%d" % (i, nh), bank_tags[(2 * i + nh) % 8])
                 for a in range(2):
                     nc.tensor.matmul_mx(
-                        out=acc[:], lhsT=v2c[:, a, rows].bitcast(FP8X4), lhsT_scale=v2s[4 * a:P, rows],
-                        rhs=pc[a, nh][:].bitcast(FP8X4), rhs_scale=psc[a, nh][:],
+                        out=acc[:], lhsT=v2c[half][:, a, rows].bitcast(FP8X4), lhsT_scale=v2s[half][4 * a:P, rows],
+                        rhs=pc[a][:, nh * BANK:(nh + 1) * BANK].bitcast(FP8X4),
+                        rhs_scale=psc[a][:, nh * BANK:(nh + 1) * BANK],
                         start=(a == 0), stop=(a == 1))
                 nc.scalar.copy(out=e[i][:, nh * BANK:(nh + 1) * BANK], in_=acc[:])
 
         def pick(i):
-            left[i] = tile([P, PAIRS], F32, "left%d" % i, "u%d" % (i % 3))
+            left[i] = tile([P, PAIRS], F32, "left%d" % i, ("u0", "u1", "u2", "u15")[i % 4])
             nc.vector.tensor_copy(left[i][:], e[i][:].indirect(pos1_t[:]))
-            diff = tile([P, PAIRS], F32, "diff%d" % i, "u%d" % (3 + i % 2))
-            nc.vector.tensor_tensor(diff[:], e[i][:].indirect(pos2_t[:]), left[i][:], ALU.subtract)
-            th[i] = tile([P, PAIRS], F32, "th%d" % i, "u%d" % (5 + i % 2))
-            nc.scalar.activation(out=th[i][:], in_=diff[:], func=ACT.Tanh, scale=-1.0)
+            right[i] = tile([P, PAIRS], F32, "right%d" % i, "u%d" % (12 + i % 3))
+            nc.vector.tensor_copy(right[i][:], e[i][:].indirect(pos2_t[:]))
 
-        def finish(i):
+        def compare(i, engine, diff):
+            engine.tensor_tensor(diff, left[i][:], right[i][:], ALU.subtract)
+            th[i] = tile([P, PAIRS], F32, "th%d" % i, ("u5", "u6", "t1_0")[i % 3])
+            nc.scalar.activation(out=th[i][:], in_=diff, func=ACT.Tanh)
+
+        def finish(i, engine):
             prod = tile([P, PAIRS], F32, "prod%d" % i, "u%d" % (7 + i % 2))
-            nc.vector.tensor_tensor(prod[:], th[i][:], left[i][:], ALU.mult)
+            engine.tensor_tensor(prod[:], th[i][:], left[i][:], ALU.mult)
             res = tile([P, PAIRS], F32, "res%d" % i, "u%d" % (9 + i % 3))
-            nc.scalar.activation(out=res[:], in_=prod[:], func=ACT.Identity, bias=bed_t[:, i:i + 1])
+            if i + 1 < n_tiles:
+                nc.scalar.activation(out=res[:], in_=prod[:], func=ACT.Identity, bias=bed_t[:, i:i + 1])
+            else:
+                nc.vector.tensor_scalar(res[:], prod[:], bed_t[:, i:i + 1], None, ALU.add)
             nc.sync.dma_start(out[i * P:(i + 1) * P, :], res[:])
 
         n_tiles = S2 // P
@@ -310,6 +354,12 @@ def tile_list_potash_face_compare_kernel(
             if i + 1 < n_tiles:
                 scores(i + 1)
             pick(i)
-            if i > 0:
-                finish(i - 1)
-        finish(n_tiles - 1)
+            if i < SUB_TILES:
+                compare(i, nc.gpsimd, tile([P, PAIRS], F32, "diff%d" % i, "u%d" % (3 + i % 2))[:])
+            if 0 < i <= MUL_TILES:
+                finish(i - 1, nc.gpsimd)
+        last_diffs = tile([P, n_tiles - SUB_TILES, PAIRS], F32, "last_diffs", "raw%d" % ((n_tiles - 1) % 4))
+        for i in range(SUB_TILES, n_tiles):
+            compare(i, nc.vector, last_diffs[:, i - SUB_TILES, :])
+        for i in range(MUL_TILES, n_tiles):
+            finish(i, nc.vector)

@@ -22,8 +22,10 @@ PACK = 4
 KP = P * PACK
 BANK = 512
 PIECE = 128
+AHEAD = 3
+E_SLOTS = ("raw0", "raw1", "raw2", "raw3", "planes10", "planes00", "planes01", "grp0")
 SUB_TILES = 6
-MUL_TILES = 4
+MUL_TILES = 5
 LAST_SCALAR_COLS = 640
 
 
@@ -77,9 +79,9 @@ def tile_list_potash_face_compare_kernel(
             nc.sync.dma_start(t[:].bitcast(I32), src)
             return t
 
-        def load_wear(b, jh):
-            t = tile([P, PACK, S // 2], F32, "wear%d%d" % (b, jh))
-            src = wear[b * KP:(b + 1) * KP, jh * (S // 2):(jh + 1) * (S // 2)]
+        def load_wear(b, jh, width):
+            t = tile([P, PACK, width], F32, "wear%d%d" % (b, jh))
+            src = wear[b * KP:(b + 1) * KP, jh * width:(jh + 1) * width]
             nc.sync.dma_start(t[:], src.rearrange("(p t) j -> p t j", t=PACK))
             return t
 
@@ -88,59 +90,67 @@ def tile_list_potash_face_compare_kernel(
             nc.sync.dma_start(pg[:], page0[b * KP:(b + 1) * KP, :].rearrange("(p t) n -> t p n", t=PACK)[t])
             return pg
 
-        wg = tile([P, PACK, S], F32, "wg")
-
-        def load_wgs(t0, t1):
-            src = wgs.rearrange("(q t) j -> q t j", t=PACK)[:, t0:t1, :]
-            for g in (0, 2, 1, 3):
-                nc.sync.dma_start(wg[32 * g:32 * g + 32, t0:t1, :], src)
-
         ts = tile([P, 2, T], U8, "ts")
         w2s = tile([P, 2, H], U8, "w2s")
         t2s = tile([P, T3], U8, "t2s")
         nc.vector.memset(ts[:].bitcast(I32), 0)
         nc.vector.memset(t2s[:].bitcast(I32), 0)
         nc.gpsimd.memset(w2s[:].bitcast(I32), 0)
+        ident = tile([P, P], F32, "ident")
+        make_identity(nc, ident[:])
         for q in range(4):
             nc.gpsimd.dma_start(
                 w2s[32 * q:32 * q + 4, :, :].bitcast(I32),
                 w2_scales.bitcast(I32)[:, 4 * q:4 * q + 4, :].rearrange("a r t -> r a t"))
-        ident = tile([P, P], F32, "ident")
-        make_identity(nc, ident[:])
 
         offs_t = load_list(offs, "offs_t")
         offs3_t = load_list(offs3, "offs3_t")
         offs2_t = load_list(offs2, "offs2_t")
         pos1_t = load_list(pos1, "pos1_t")
         pos2_t = load_list(pos2, "pos2_t")
-        tab = [load_table(tab_words, a, "tab%d" % a) for a in range(2)]
+        tab = [load_table(tab_words, 0, "tab0")]
+        wgs_rows = tile([P, S], F32, "wgs_rows", "h0")
+        nc.sync.dma_start(wgs_rows[:], wgs)
+        tab.append(load_table(tab_words, 1, "tab1"))
         w2t = {0: load_w2(0)}
         for q in range(4):
             nc.sync.dma_start(
                 ts[32 * q:32 * q + 4, :, :].bitcast(I32),
                 tab_scales.bitcast(I32)[:, 4 * q:4 * q + 4, :].rearrange("a r t -> r a t"))
         raw = {(0, 0): load_w1(0, 0)}
+        raw[1, 0] = load_w1(1, 0, 2)
         for q in range(4):
             nc.sync.dma_start(
                 t2s[32 * q:32 * q + 8, :].bitcast(I32),
                 tab2_scales.bitcast(I32)[:, 4 * q:4 * q + 4, :])
-        raw[1, 0] = load_w1(1, 0, 2)
-        weart = {(0, jh): load_wear(0, jh) for jh in range(2)}
+        weart = {(0, 0): load_wear(0, 0, S)}
         raw[0, 1] = load_w1(0, 1)
         page = {(0, 0): load_page(0, 0)}
-        load_wgs(0, 1)
         page[0, 1] = load_page(0, 1)
-        load_wgs(1, 2)
         raw[1, 1] = load_w1(1, 1)
         w2t[1] = load_w2(1)
         page[0, 2] = load_page(0, 2)
-        load_wgs(2, 3)
-        for jh in range(2):
-            weart[1, jh] = load_wear(1, jh)
+        weart[1, 0] = load_wear(1, 0, S)
         page[0, 3] = load_page(0, 3)
-        load_wgs(3, 4)
         for t in range(PACK):
             page[1, t] = load_page(1, t)
+
+        wgs_turned = bank("wgs_turned", "H0")
+        for jb in range(4):
+            nc.tensor.transpose(wgs_turned[:, jb * P:(jb + 1) * P], wgs_rows[:, jb * P:(jb + 1) * P], ident[:])
+        dealt = []
+        for jb in range(4):
+            d = tile([P, PACK, 4, 32], F32, "dealt%d" % jb, "u%d" % (8 + jb))
+            src = wgs_turned[:, jb * P:(jb + 1) * P].rearrange("j (q t) -> j t q", t=PACK)
+            nc.scalar.copy(out=d[:], in_=src.unsqueeze(2).to_broadcast([P, PACK, 4, 32]))
+            dealt.append(d)
+        wg = tile([P, PACK, S], F32, "wg")
+        for t in range(PACK):
+            back = bank("wgs_back%d" % t, ("A0", "A1", "H1", "W1")[t])
+            for jb in range(4):
+                nc.tensor.transpose(back[:, jb * P:(jb + 1) * P],
+                                    dealt[jb][:, t, :, :].rearrange("j g q -> j (g q)"), ident[:])
+            nc.scalar.copy(out=wg[:, t, :], in_=back[:])
 
         vc, vs = [], []
         for a in range(2):
@@ -150,10 +160,6 @@ def tile_list_potash_face_compare_kernel(
             nc.vector.tensor_copy(s[:], ts[:, a, :].indirect(offs_t[:]))
             vc.append(c)
             vs.append(s)
-
-        bed_t = tile([P, S2 // P], F32, "bed_t")
-        with nc.allow_non_contiguous_dma(reason="one value of bed to each partition and row tile"):
-            nc.sync.dma_start(bed_t[:], bed.rearrange("(i p) -> p i", p=P))
 
         w1c, w1s, bT, t2T, hh = {}, {}, {}, {}, {}
 
@@ -195,7 +201,7 @@ def tile_list_potash_face_compare_kernel(
             wT[b, jb] = bank("W%d%d" % (b, jb), (("B0", "B1", "W0", "W1"), ("W0", "W1", "A0", "A1"))[b][jb])
             for t in range(PACK):
                 nc.tensor.transpose(wT[b, jb][:, t * P:(t + 1) * P],
-                                    weart[b, jb // 2][:, t, jb % 2 * P:(jb % 2 + 1) * P], ident[:])
+                                    weart[b, 0][:, t, jb * P:(jb + 1) * P], ident[:])
 
         def bounded_part(b, jb):
             if (b, jb) == (0, 3):
@@ -234,7 +240,7 @@ def tile_list_potash_face_compare_kernel(
             interleave(engine_copy, pgrp[a][:, nh * BANK:(nh + 1) * BANK, :], planes[a, nh], c0, c1)
 
         def quantise_page(a):
-            pc[a] = tile([P, T2], U32, "pc%d" % a, "wear%d1" % a)
+            pc[a] = tile([P, T2], U32, "pc%d" % a)
             psc[a] = tile([P, T2], U8, "psc%d" % a)
             nc.vector.quantize_mx(out=pc[a][:].bitcast(FP8X4), scales=psc[a][:],
                                   in_=pgrp[a][:].rearrange("p c t -> p (c t)"))
@@ -258,12 +264,10 @@ def tile_list_potash_face_compare_kernel(
         for jb in range(4):
             w1_pass(0, jb, 0)
         gather_v2_scales(0, tile([P, 512], U8, "v2s0", "grp1"))
-        turn_wear(0, 0)
-        turn_wear(0, 1)
         for jb in range(4):
             w1_pass(0, jb, 1)
-        turn_wear(0, 2)
-        turn_wear(0, 3)
+        for jb in range(4):
+            turn_wear(0, jb)
         for jb in range(4):
             bounded_part(0, jb)
         gather_v2_scales(1, late.tile([P, 512], U8, name="v2s1", offset=0, align_bytes=64))
@@ -294,6 +298,9 @@ def tile_list_potash_face_compare_kernel(
         scatter(1, 1)
         make_h(1, 2, "H0", "h1")
         scatter(1, 2)
+        bed_t = tile([P, S2 // P], F32, "bed_t", "h1")
+        with nc.allow_non_contiguous_dma(reason="one value of bed to each partition and row tile"):
+            nc.sync.dma_start(bed_t[:], bed.rearrange("(i p) -> p i", p=P))
         pgrp[0] = tile([P, T2, PACK], BF16, "pgrp0", "wear00")
         round_page(0, 0, nc.scalar.copy, 0, BANK)
         make_h(1, 3, "H1", "planes00")
@@ -316,7 +323,7 @@ def tile_list_potash_face_compare_kernel(
 
         def scores(i):
             half, rows = i // 4, slice(i % 4 * P, (i % 4 + 1) * P)
-            e[i] = tile([P, T2], F32, "e%d" % i, "raw%d" % (i % 4))
+            e[i] = tile([P, T2], F32, "e%d" % i, E_SLOTS[i])
             for nh in range(2):
                 acc = bank("E%d%d" % (i, nh), bank_tags[(2 * i + nh) % 8])
                 for a in range(2):
@@ -328,20 +335,20 @@ def tile_list_potash_face_compare_kernel(
                 nc.scalar.copy(out=e[i][:, nh * BANK:(nh + 1) * BANK], in_=acc[:])
 
         def pick(i):
-            left[i] = tile([P, PAIRS], F32, "left%d" % i, ("u0", "u1", "u2", "u15")[i % 4])
-            nc.vector.tensor_copy(left[i][:], e[i][:].indirect(pos1_t[:]))
-            right[i] = tile([P, PAIRS], F32, "right%d" % i, "u%d" % (12 + i % 3))
-            nc.vector.tensor_copy(right[i][:], e[i][:].indirect(pos2_t[:]))
+            pair = tile([P, 2, PAIRS], F32, "pair%d" % i, "page%d%d" % (i // 4, i % 4))
+            left[i], right[i] = pair[:, 0, :], pair[:, 1, :]
+            nc.vector.tensor_copy(left[i], e[i][:].indirect(pos1_t[:]))
+            nc.vector.tensor_copy(right[i], e[i][:].indirect(pos2_t[:]))
 
         def compare(i, engine, diff):
-            engine.tensor_tensor(diff, left[i][:], right[i][:], ALU.subtract)
-            th[i] = tile([P, PAIRS], F32, "th%d" % i, ("u5", "u6", "t1_0")[i % 3])
+            engine.tensor_tensor(diff, left[i], right[i], ALU.subtract)
+            th[i] = tile([P, PAIRS], F32, "th%d" % i, "u%d" % (12 + i % 4))
             nc.scalar.activation(out=th[i][:], in_=diff, func=ACT.Tanh)
 
         def finish(i, engine):
-            prod = tile([P, PAIRS], F32, "prod%d" % i, "u%d" % (7 + i % 2))
-            engine.tensor_tensor(prod[:], th[i][:], left[i][:], ALU.mult)
-            res = tile([P, PAIRS], F32, "res%d" % i, "u%d" % (9 + i % 3))
+            prod = tile([P, PAIRS], F32, "prod%d" % i, "u%d" % (3 + i % 3))
+            engine.tensor_tensor(prod[:], th[i][:], left[i], ALU.mult)
+            res = tile([P, PAIRS], F32, "res%d" % i, "u%d" % (6 + i % 4))
             if i + 1 < n_tiles:
                 nc.scalar.activation(out=res[:], in_=prod[:], func=ACT.Identity, bias=bed_t[:, i:i + 1])
             else:
@@ -349,16 +356,17 @@ def tile_list_potash_face_compare_kernel(
             nc.sync.dma_start(out[i * P:(i + 1) * P, :], res[:])
 
         n_tiles = S2 // P
-        scores(0)
+        for i in range(AHEAD):
+            scores(i)
         for i in range(n_tiles):
-            if i + 1 < n_tiles:
-                scores(i + 1)
+            if i + AHEAD < n_tiles:
+                scores(i + AHEAD)
             pick(i)
             if i < SUB_TILES:
-                compare(i, nc.gpsimd, tile([P, PAIRS], F32, "diff%d" % i, "u%d" % (3 + i % 2))[:])
+                compare(i, nc.gpsimd, tile([P, PAIRS], F32, "diff%d" % i, "u%d" % (i % 3))[:])
             if 0 < i <= MUL_TILES:
                 finish(i - 1, nc.gpsimd)
-        last_diffs = tile([P, n_tiles - SUB_TILES, PAIRS], F32, "last_diffs", "raw%d" % ((n_tiles - 1) % 4))
+        last_diffs = tile([P, n_tiles - SUB_TILES, PAIRS], F32, "last_diffs", "u%d" % (12 + (MUL_TILES - 1) % 4))
         for i in range(SUB_TILES, n_tiles):
             compare(i, nc.vector, last_diffs[:, i - SUB_TILES, :])
         for i in range(MUL_TILES, n_tiles):

from contextlib import ExitStack

import concourse.mybir as mybir
from concourse.masks import make_identity

K, T, S, H, T2, S2, T3, PAIRS = 1024, 2048, 512, 1024, 1024, 1024, 2048, 512
FLOPS = 2 * K * H * S * 2 + 2 * H * S2 * T2

F32 = mybir.dt.float32
BF16 = mybir.dt.bfloat16
I32 = mybir.dt.int32
U32 = mybir.dt.uint32
U16 = mybir.dt.uint16
U8 = mybir.dt.uint8
FP8X4 = mybir.dt.float8_e4m3fn_x4
FP4X4 = mybir.dt.float4_e2m1fn_x4
ACT = mybir.ActivationFunctionType
ALU = mybir.AluOpType

P = 128
PACK = 4
KP = P * PACK
BANK = 512
PIECE = 128
AHEAD = 3
E_SLOTS = ("raw0", "raw1", "raw2", "raw3", "planes10", "planes00", "planes01", "grp0")
SUB_TILES = 6
MUL_TILES = 5
LAST_SCALAR_COLS = 640


def interleave(engine_copy, grouped, planes, c0, c1):
    engine_copy(
        out=grouped[:, c0:c1, :].rearrange("p (c i) t -> p c t i", i=4),
        in_=planes[:, :, c0:c1].rearrange("p t (c i) -> p c t i", i=4),
    )


def tile_list_potash_face_compare_kernel(
    tc, tab_words, tab_scales, offs, w1, w2_words, w2_scales, wear, page0, wgs, offs3,
    tab2_words, tab2_scales, offs2, pos1, pos2, bed, out,
):
    nc = tc.nc
    with ExitStack() as ctx:
        lists = ctx.enter_context(tc.tile_pool(name="lists", bufs=1))
        sb = ctx.enter_context(tc.tile_pool(name="sb", bufs=1))
        late = ctx.enter_context(tc.tile_pool(name="late", bufs=1))
        ps = ctx.enter_context(tc.psum_pool(name="ps", bufs=1))

        def tile(shape, dtype, name, tag=None):
            return sb.tile(shape, dtype, name=name, tag=tag or name, align_bytes=64)

        def bank(name, tag):
            return ps.tile([P, BANK], F32, name=name, tag=tag)

        def load_list(src, name):
            t = lists.tile([P, src.shape[1]], U16, name=name)
            nc.sync.dma_start(t[:], src)
            return t

        def load_table(words, a, name):
            t = tile([P, T], I32, name, "table%d" % a)
            nc.sync.dma_start(t[:], words[a].rearrange("p t i -> p (t i)").bitcast(I32))
            return t

        def load_w1(a, b, pieces=1):
            src = w1[a * KP:(a + 1) * KP, b * BANK:(b + 1) * BANK].rearrange("(p j) c -> p j c", j=PACK)
            width = BANK // pieces
            tiles = []
            for n in range(pieces):
                t = tile([P, PACK, width], F32, "w1_raw%d%d%d" % (a, b, n), "raw%d" % (2 * b + a + 4 * n))
                nc.sync.dma_start(t[:], src[:, :, n * width:(n + 1) * width])
                tiles.append(t)
            return tiles

        def load_w2(b):
            t = tile([P, 2, 2 * BANK], U8, "w2_%d" % b)
            src = w2_words.bitcast(I32)[:, :, b * 256:(b + 1) * 256].rearrange("a p c -> p a c")
            nc.sync.dma_start(t[:].bitcast(I32), src)
            return t

        def load_wear(b, jh, width):
            t = tile([P, PACK, width], F32, "wear%d%d" % (b, jh))
            src = wear[b * KP:(b + 1) * KP, jh * width:(jh + 1) * width]
            nc.sync.dma_start(t[:], src.rearrange("(p t) j -> p t j", t=PACK))
            return t

        def load_page(b, t):
            pg = tile([P, T2], F32, "page%d%d" % (b, t))
            nc.sync.dma_start(pg[:], page0[b * KP:(b + 1) * KP, :].rearrange("(p t) n -> t p n", t=PACK)[t])
            return pg

        ts = tile([P, 2, T], U8, "ts")
        w2s = tile([P, 2, H], U8, "w2s")
        t2s = tile([P, T3], U8, "t2s")
        nc.vector.memset(ts[:].bitcast(I32), 0)
        nc.vector.memset(t2s[:].bitcast(I32), 0)
        nc.gpsimd.memset(w2s[:].bitcast(I32), 0)
        ident = tile([P, P], F32, "ident")
        make_identity(nc, ident[:])
        for q in range(4):
            nc.gpsimd.dma_start(
                w2s[32 * q:32 * q + 4, :, :].bitcast(I32),
                w2_scales.bitcast(I32)[:, 4 * q:4 * q + 4, :].rearrange("a r t -> r a t"))

        offs_t = load_list(offs, "offs_t")
        offs3_t = load_list(offs3, "offs3_t")
        offs2_t = load_list(offs2, "offs2_t")
        pos1_t = load_list(pos1, "pos1_t")
        pos2_t = load_list(pos2, "pos2_t")
        tab = [load_table(tab_words, 0, "tab0")]
        wgs_rows = tile([P, S], F32, "wgs_rows", "h0")
        nc.sync.dma_start(wgs_rows[:], wgs)
        tab.append(load_table(tab_words, 1, "tab1"))
        w2t = {0: load_w2(0)}
        for q in range(4):
            nc.sync.dma_start(
                ts[32 * q:32 * q + 4, :, :].bitcast(I32),
                tab_scales.bitcast(I32)[:, 4 * q:4 * q + 4, :].rearrange("a r t -> r a t"))
        raw = {(0, 0): load_w1(0, 0)}
        raw[1, 0] = load_w1(1, 0, 2)
        for q in range(4):
            nc.sync.dma_start(
                t2s[32 * q:32 * q + 8, :].bitcast(I32),
                tab2_scales.bitcast(I32)[:, 4 * q:4 * q + 4, :])
        weart = {(0, 0): load_wear(0, 0, S)}
        raw[0, 1] = load_w1(0, 1)
        page = {(0, 0): load_page(0, 0)}
        page[0, 1] = load_page(0, 1)
        raw[1, 1] = load_w1(1, 1)
        w2t[1] = load_w2(1)
        page[0, 2] = load_page(0, 2)
        weart[1, 0] = load_wear(1, 0, S)
        page[0, 3] = load_page(0, 3)
        for t in range(PACK):
            page[1, t] = load_page(1, t)

        wgs_turned = bank("wgs_turned", "H0")
        for jb in range(4):
            nc.tensor.transpose(wgs_turned[:, jb * P:(jb + 1) * P], wgs_rows[:, jb * P:(jb + 1) * P], ident[:])
        dealt = []
        for jb in range(4):
            d = tile([P, PACK, 4, 32], F32, "dealt%d" % jb, "u%d" % (8 + jb))
            src = wgs_turned[:, jb * P:(jb + 1) * P].rearrange("j (q t) -> j t q", t=PACK)
            nc.scalar.copy(out=d[:], in_=src.unsqueeze(2).to_broadcast([P, PACK, 4, 32]))
            dealt.append(d)
        wg = tile([P, PACK, S], F32, "wg")
        for t in range(PACK):
            back = bank("wgs_back%d" % t, ("A0", "A1", "H1", "W1")[t])
            for jb in range(4):
                nc.tensor.transpose(back[:, jb * P:(jb + 1) * P],
                                    dealt[jb][:, t, :, :].rearrange("j g q -> j (g q)"), ident[:])
            nc.scalar.copy(out=wg[:, t, :], in_=back[:])

        vc, vs = [], []
        for a in range(2):
            c = tile([P, S], U32, "vc%d" % a)
            nc.vector.tensor_copy(c[:], tab[a][:].bitcast(U32).indirect(offs_t[:]))
            s = tile([P, S], U8, "vs%d" % a)
            nc.vector.tensor_copy(s[:], ts[:, a, :].indirect(offs_t[:]))
            vc.append(c)
            vs.append(s)

        w1c, w1s, bT, t2T, hh = {}, {}, {}, {}, {}

        def quantise_w1(a, b, engine_copy, piece, grp):
            width = BANK // len(raw[a, b])
            for n, src in enumerate(raw[a, b]):
                for c0 in range(0, width, piece):
                    interleave(engine_copy, grp[:, n * width:(n + 1) * width, :], src, c0, c0 + piece)
            w1c[a, b] = tile([P, BANK], U32, "w1c%d%d" % (a, b))
            w1s[a, b] = tile([P, BANK], U8, "w1s%d%d" % (a, b))
            nc.vector.quantize_mx(out=w1c[a, b][:].bitcast(FP8X4), scales=w1s[a, b][:],
                                  in_=grp[:].rearrange("p c t -> p (c t)"))

        def plain_part(b, jb):
            cols = slice(jb * P, (jb + 1) * P)
            acc = bank("B%d%d" % (b, jb), (("B0", "B1", "W0", "W1"), ("W0", "W1", "A0", "A1"))[b][jb])
            for a in range(2):
                nc.tensor.matmul_mx(
                    out=acc[:], lhsT=vc[a][:, cols].bitcast(FP8X4), lhsT_scale=vs[a][:, cols],
                    rhs=w2t[b][:, a, :].bitcast(FP4X4), rhs_scale=w2s[:, a, b * BANK:(b + 1) * BANK],
                    start=(a == 0), stop=(a == 1))
            bT[b, jb] = tile([P, PACK, P], F32, "bT%d%d" % (b, jb), "u%d" % (8 * b + jb))
            nc.scalar.copy(out=bT[b, jb][:], in_=acc[:].rearrange("j (p t) -> j t p", t=PACK))

        accA = {}

        def w1_pass(b, jb, a):
            cols = slice(jb * P, (jb + 1) * P)
            if a == 0:
                accA[b, jb] = bank("A%d%d" % (b, jb), (("A0", "A1", "H0", "H1"), ("B0", "B1", "H1", "H0"))[b][jb])
            nc.tensor.matmul_mx(
                out=accA[b, jb][:], lhsT=vc[a][:, cols].bitcast(FP8X4), lhsT_scale=vs[a][:, cols],
                rhs=w1c[a, b][:].bitcast(FP8X4), rhs_scale=w1s[a, b][:],
                start=(a == 0), stop=(a == 1))

        wT = {}

        def turn_wear(b, jb):
            wT[b, jb] = bank("W%d%d" % (b, jb), (("B0", "B1", "W0", "W1"), ("W0", "W1", "A0", "A1"))[b][jb])
            for t in range(PACK):
                nc.tensor.transpose(wT[b, jb][:, t * P:(t + 1) * P],
                                    weart[b, 0][:, t, jb * P:(jb + 1) * P], ident[:])

        def bounded_part(b, jb):
            if (b, jb) == (0, 3):
                t1 = late.tile([P, PACK, P], F32, name="t1_03", offset=0, align_bytes=64)
            else:
                t1 = tile([P, PACK, P], F32, "t1_%d%d" % (b, jb), "t1_%d" % jb)
            nc.scalar.activation(out=t1[:], in_=accA[b, jb][:].rearrange("j (p t) -> j t p", t=PACK), func=ACT.Tanh)
            t2T[b, jb] = tile([P, PACK, P], F32, "t2_%d%d" % (b, jb), "u%d" % (8 * b + 4 + jb))
            nc.vector.tensor_tensor(t2T[b, jb][:].rearrange("j t p -> j (t p)"),
                                    t1[:].rearrange("j t p -> j (t p)"), wT[b, jb][:], ALU.mult)

        def make_h(b, t, bank_tag, h_tag):
            acc = bank("H%d%d" % (b, t), bank_tag)
            for jb in range(4):
                cols = slice(jb * P, (jb + 1) * P)
                nc.tensor.matmul(acc[:, cols], lhsT=bT[b, jb][:, t, :], rhs=ident[:],
                                 is_transpose=True, start=True, stop=False)
                nc.tensor.matmul(acc[:, cols], lhsT=t2T[b, jb][:, t, :], rhs=ident[:],
                                 is_transpose=True, start=False, stop=True)
            hh[b, t] = tile([P, S], F32, "h%d%d" % (b, t), h_tag)
            nc.scalar.copy(out=hh[b, t][:], in_=acc[:])

        planes = {}

        def scatter(b, t):
            nc.vector.tensor_tensor(page[b, t][:].indirect(offs3_t[:]), hh[b, t][:], wg[:, t, :], ALU.mult)
            for nh in range(2):
                if t == 0:
                    planes[b, nh] = tile([P, PACK, BANK], F32, "planes%d%d" % (b, nh))
                if (b, t) != (1, 3):
                    nc.sync.dma_start(planes[b, nh][:, t, :], page[b, t][:, nh * BANK:(nh + 1) * BANK])

        pgrp, pc, psc = {}, {}, {}

        def round_page(a, nh, engine_copy, c0, c1):
            interleave(engine_copy, pgrp[a][:, nh * BANK:(nh + 1) * BANK, :], planes[a, nh], c0, c1)

        def quantise_page(a):
            pc[a] = tile([P, T2], U32, "pc%d" % a)
            psc[a] = tile([P, T2], U8, "psc%d" % a)
            nc.vector.quantize_mx(out=pc[a][:].bitcast(FP8X4), scales=psc[a][:],
                                  in_=pgrp[a][:].rearrange("p c t -> p (c t)"))

        v2c, v2s = {}, {}

        def gather_v2_scales(half, dst):
            v2s[half] = dst
            nc.vector.tensor_copy(v2s[half][:], t2s[:].indirect(offs2_t[:, half * 32:(half + 1) * 32]))

        def gather_v2_words(half, tag):
            v2c[half] = tile([P, 2, 512], U32, "v2c%d" % half, tag)
            for a in range(2):
                nc.vector.tensor_copy(
                    v2c[half][:, a, :], tab2[a][:].bitcast(U32).indirect(offs2_t[:, half * 32:(half + 1) * 32]))

        quantise_w1(0, 0, nc.vector.tensor_copy, BANK, tile([P, BANK, PACK], BF16, "grp00", "grp0"))
        quantise_w1(1, 0, nc.vector.tensor_copy, BANK // 2, tile([P, BANK, PACK], BF16, "grp10", "grp1"))
        for jb in range(4):
            plain_part(0, jb)
        for jb in range(4):
            w1_pass(0, jb, 0)
        gather_v2_scales(0, tile([P, 512], U8, "v2s0", "grp1"))
        for jb in range(4):
            w1_pass(0, jb, 1)
        for jb in range(4):
            turn_wear(0, jb)
        for jb in range(4):
            bounded_part(0, jb)
        gather_v2_scales(1, late.tile([P, 512], U8, name="v2s1", offset=0, align_bytes=64))
        make_h(0, 0, "A0", "h0")
        scatter(0, 0)
        quantise_w1(0, 1, nc.scalar.copy, PIECE, late.tile([P, BANK, PACK], BF16, name="grp01", offset=512, align_bytes=64))
        make_h(0, 1, "A1", "raw2")
        scatter(0, 1)
        quantise_w1(1, 1, nc.scalar.copy, PIECE, tile([P, BANK, PACK], BF16, "grp11", "grp0"))
        make_h(0, 2, "H0", "raw3")
        scatter(0, 2)
        for jb in range(4):
            plain_part(1, jb)
        for jb in range(4):
            w1_pass(1, jb, 0)
        for jb in range(4):
            w1_pass(1, jb, 1)
        for jb in range(4):
            turn_wear(1, jb)
            bounded_part(1, jb)
        make_h(0, 3, "H1", "table0")
        scatter(0, 3)
        tab2 = [load_table(tab2_words, 0, "tab2_0")]
        make_h(1, 0, "A1", "table1")
        scatter(1, 0)
        tab2.append(load_table(tab2_words, 1, "tab2_1"))
        make_h(1, 1, "A0", "h0")
        scatter(1, 1)
        make_h(1, 2, "H0", "h1")
        scatter(1, 2)
        bed_t = tile([P, S2 // P], F32, "bed_t", "h1")
        with nc.allow_non_contiguous_dma(reason="one value of bed to each partition and row tile"):
            nc.sync.dma_start(bed_t[:], bed.rearrange("(i p) -> p i", p=P))
        pgrp[0] = tile([P, T2, PACK], BF16, "pgrp0", "wear00")
        round_page(0, 0, nc.scalar.copy, 0, BANK)
        make_h(1, 3, "H1", "planes00")
        round_page(0, 1, nc.scalar.copy, 0, BANK)
        quantise_page(0)
        scatter(1, 3)

        pgrp[1] = tile([P, T2, PACK], BF16, "pgrp1", "wear10")
        for nh in range(2):
            nc.vector.tensor_copy(out=planes[1, nh][:, 3, :], in_=page[1, 3][:, nh * BANK:(nh + 1) * BANK])
        round_page(1, 0, nc.scalar.copy, 0, BANK)
        round_page(1, 1, nc.scalar.copy, 0, LAST_SCALAR_COLS - BANK)
        round_page(1, 1, nc.vector.tensor_copy, LAST_SCALAR_COLS - BANK, BANK)
        gather_v2_words(0, "wg")
        quantise_page(1)
        gather_v2_words(1, "wear10")

        bank_tags = ("B0", "B1", "W0", "W1", "A0", "A1", "H1", "H0")
        e, left, right, th = {}, {}, {}, {}

        def scores(i):
            half, rows = i // 4, slice(i % 4 * P, (i % 4 + 1) * P)
            e[i] = tile([P, T2], F32, "e%d" % i, E_SLOTS[i])
            for nh in range(2):
                acc = bank("E%d%d" % (i, nh), bank_tags[(2 * i + nh) % 8])
                for a in range(2):
                    nc.tensor.matmul_mx(
                        out=acc[:], lhsT=v2c[half][:, a, rows].bitcast(FP8X4), lhsT_scale=v2s[half][4 * a:P, rows],
                        rhs=pc[a][:, nh * BANK:(nh + 1) * BANK].bitcast(FP8X4),
                        rhs_scale=psc[a][:, nh * BANK:(nh + 1) * BANK],
                        start=(a == 0), stop=(a == 1))
                nc.scalar.copy(out=e[i][:, nh * BANK:(nh + 1) * BANK], in_=acc[:])

        def pick(i):
            pair = tile([P, 2, PAIRS], F32, "pair%d" % i, "page%d%d" % (i // 4, i % 4))
            left[i], right[i] = pair[:, 0, :], pair[:, 1, :]
            nc.vector.tensor_copy(left[i], e[i][:].indirect(pos1_t[:]))
            nc.vector.tensor_copy(right[i], e[i][:].indirect(pos2_t[:]))

        def compare(i, engine, diff):
            engine.tensor_tensor(diff, left[i], right[i], ALU.subtract)
            th[i] = tile([P, PAIRS], F32, "th%d" % i, "u%d" % (12 + i % 4))
            nc.scalar.activation(out=th[i][:], in_=diff, func=ACT.Tanh)

        def finish(i, engine):
            prod = tile([P, PAIRS], F32, "prod%d" % i, "u%d" % (3 + i % 3))
            engine.tensor_tensor(prod[:], th[i][:], left[i], ALU.mult)
            res = tile([P, PAIRS], F32, "res%d" % i, "u%d" % (6 + i % 4))
            if i + 1 < n_tiles:
                nc.scalar.activation(out=res[:], in_=prod[:], func=ACT.Identity, bias=bed_t[:, i:i + 1])
            else:
                nc.vector.tensor_scalar(res[:], prod[:], bed_t[:, i:i + 1], None, ALU.add)
            nc.sync.dma_start(out[i * P:(i + 1) * P, :], res[:])

        n_tiles = S2 // P
        for i in range(AHEAD):
            scores(i)
        for i in range(n_tiles):
            if i + AHEAD < n_tiles:
                scores(i + AHEAD)
            pick(i)
            if i < SUB_TILES:
                compare(i, nc.gpsimd, tile([P, PAIRS], F32, "diff%d" % i, "u%d" % (i % 3))[:])
            if 0 < i <= MUL_TILES:
                finish(i - 1, nc.gpsimd)
        last_diffs = tile([P, n_tiles - SUB_TILES, PAIRS], F32, "last_diffs", "u%d" % (12 + (MUL_TILES - 1) % 4))
        for i in range(SUB_TILES, n_tiles):
            compare(i, nc.vector, last_diffs[:, i - SUB_TILES, :])
        for i in range(MUL_TILES, n_tiles):
            finish(i, nc.vector)
